import numpy as np, ml_dtypes
CORES = [8,136,40,168]
N = 4
BF = ml_dtypes.bfloat16
def gentries(a):
    return np.ascontiguousarray(a.reshape(8, 16, -1).transpose(0, 2, 1)).reshape(8, -1)
def gtable(e):
    e = np.asarray(e); return np.ascontiguousarray(e.reshape(8, -1, 16).transpose(0, 2, 1)).reshape(128, -1).astype(np.int32)
V, R, L, S = 2048, 384, 4, 2
def trees(rng, deep):
    T = N * 8; ar = np.arange(T); P = V // 2 - 1; i = np.arange(P)[:, None]
    pair = 2 * (np.argsort(rng.random((T, P)), axis=1) + 1); side = rng.integers(0, 2, (P, T))
    pick = np.where(rng.random((P, T)) < deep, i, np.minimum((rng.random((P, T)) * (i + 1)).astype(np.int64), i))
    kid = np.full((T, V), -1, np.int64); up = np.zeros((T, V), np.int64); leaf = np.zeros((T, P + 1), np.int64); cnt = np.ones((T, V), np.int64)
    for t in range(P):
        j = pick[t]; n = leaf[ar, j]; k = pair[:, t]; b = side[t]
        kid[ar, n] = k; up[ar, k] = n; up[ar, k + 1] = n
        leaf[ar, j] = k + b; leaf[ar, t + 1] = k + 1 - b
    for t in range(P - 1, -1, -1):
        k = pair[:, t]; cnt[ar, up[ar, k]] = cnt[ar, k] + cnt[ar, k + 1]
    return kid, up, cnt
def quads(rng, kid, cnt, top, drop):
    T = N * 8; Q = 4 * R; ar = np.arange(T)[:, None]; ar3 = ar[:, :, None]
    ok = cnt >= 4; order = np.argsort(~ok, axis=1, kind="stable"); num = np.sum(ok, axis=1)[:, None]
    x = order[ar, np.minimum((rng.random((T, Q)) * num).astype(np.int64), num - 1)]
    c = np.full((T, Q, 4), -1, np.int64); c[:, :, 0] = np.where(rng.random((T, Q)) < top, 0, x)
    for w in (1, 2, 3):
        k = kid[ar3, np.maximum(c, 0)]
        t = np.argmax(np.where((c >= 0) & (k >= 0), rng.random(c.shape), -1.0), axis=2)[..., None]
        k = np.take_along_axis(k, t, 2); np.put_along_axis(c, t, k, 2); c[:, :, w] = k[..., 0] + 1
    m = rng.random((T, Q, 1)) < drop
    for w in range(4):
        k = kid[ar3, c]; go = m & (k >= 0) & (rng.random(c.shape) < 0.3)
        c = np.where(go, k + rng.integers(0, 2, c.shape), c)
    return np.take_along_axis(c, np.argsort(rng.random(c.shape), axis=2), 2)
def parts(rng, deep=0.2, top=0.15, drop=0.5):
    kid, up, cnt = trees(rng, deep)
    return {"s": rng.integers(0, 256, (N, 8, 16, V)), "m": rng.integers(0, 256, (N, 8, 16, V)), "kid": kid, "up": up,
            "a": rng.integers(0, 256, (N, 8, 16, R)), "a0": rng.integers(0, 256, (N, 8, 16, R)), "lk": rng.integers(0, R, (N, 8, L, R)), "cut0": quads(rng, kid, cnt, top, drop)}
def pack(d):
    q = {}
    for k in ("s", "m", "kid", "up", "a", "a0", "lk", "cut0"):
        v = d[k]
        if k in ("kid", "up"): q[k] = np.ascontiguousarray(v.reshape(N, 8, V)).astype(np.int32)
        elif k in ("lk", "cut0"): q[k] = np.stack([gtable(x) for x in v.reshape(N, 8, -1)])
        else: q[k] = np.ascontiguousarray(v.reshape(N, 128, -1)).astype(np.float32).astype(BF)
    return q
def setup_inputs(rng):
    return pack(parts(rng))
def setup_inputs_ties(rng):
    d = parts(rng, 0.2, 0.3, 0.4)
    d["a"] = rng.integers(1, 3, (N, 8, 16, R)); d["a0"] = rng.integers(1, 3, (N, 8, 16, R))
    d["s"] = np.repeat(rng.integers(0, 3, (N, 8, 1, V)) * rng.choice(np.array([1, 7, 100]), (N, 8, 1, 1)), 16, axis=2)
    d["s"][:, 3] = 7; d["s"][:, 5] = np.where(rng.random((N, 16, V)) < 0.5, 1, 2)
    return pack(d)
def setup_inputs_deep(rng):
    T = N * 8; Q = 4 * R; deep = rng.choice(np.array([0.0, 0.9, 1.0]), (1, T)); deep[0, 0] = 1.0; deep[0, T - 1] = 0.0
    d = parts(rng, deep, 0.05, 0.3); n = np.arange(V)[None, :]
    leaf = np.argsort(np.where((d["kid"] < 0) & (n != 1), n, V + n), axis=1)[:, :V // 2]
    at = rng.integers(0, V // 2 - 3, (T, Q)); at[:, 0] = 0; at[:, 1] = V // 2 - 4
    m = rng.random((T, Q)) < 0.4; m[:, :2] = True
    four = leaf[np.arange(T)[:, None, None], at[:, :, None] + np.arange(4)]
    four = np.take_along_axis(four, np.argsort(rng.random(four.shape), axis=2), 2)
    d["cut0"] = np.where(m[:, :, None], four, d["cut0"])
    return pack(d)
def top_end(rng, d, g):
    ar = np.arange(N); c = d["cut0"].reshape(N, 8, R, 4, 4).copy(); k = d["kid"].reshape(N, 8, V)[:, g]; u = d["up"].reshape(N, 8, V)[:, g]
    q = c[:, g].reshape(N, 4 * R, 4); sib = np.any(q[..., None, :] == (q ^ 1)[..., :, None], axis=3)
    q = np.take_along_axis(q, np.argsort(~sib, axis=2, kind="stable"), 2)
    inner = k[ar[:, None, None], q] >= 0; good = (np.sum(sib, axis=2) == 2) & inner[..., 2] & inner[..., 3]
    p = q[ar, np.argmax(good, axis=1)]
    c[:, g] = q.reshape(N, R, 4, 4); c[:, g, ::2, 0] = p[:, None, :]; d["cut0"] = c
    j = rng.integers(0, 16, (N, V))
    j[ar, p[:, 0]] = 2; j[ar, p[:, 1]] = 2; j[ar, u[ar, p[:, 0]]] = 2; j[ar, p[:, 2]] = 1; j[ar, p[:, 3]] = 1
    d["s"][:, g] = 255 - (np.arange(16)[None, :, None] == j[:, None, :]).astype(np.int64)
    d["a"][:, g] = rng.integers(254, 256, (N, 16, R)); d["a"][:, g, 12:] = 255; d["a"][:, g, 1, ::2] = 254; d["a"][:, g, 2, ::2] = 255
    d["a0"][:, g] = rng.integers(0, 2, (N, 16, R))
def setup_inputs_ends(rng):
    d = parts(rng)
    for k in ("s", "m", "a", "a0"):
        e = rng.random(d[k].shape); d[k] = np.where(e < 0.4, 255, np.where(e < 0.7, 0, d[k]))
    for k in ("s", "m", "a"): d[k][:, 0] = 255
    d["a"][:, 1, :, ::2] = 0; d["s"][:, 2] = 0
    d["lk"][:, ::2] = rng.choice(np.array([0, R - 1]), (N, 4, L, R))
    top_end(rng, d, 7)
    return pack(d)
def setup_inputs_alike(rng):
    d = parts(rng, 0.0, 1.0, 0.2)
    d["lk"][:, 1::2] = rng.integers(0, R, (N, 4, 1, 1))
    c = d["cut0"].reshape(N, 8, R, 16).copy(); c[:, ::2] = c[:, ::2, :1].copy(); d["cut0"] = c
    d["a"][:, :4] = np.repeat(d["a"][:, :4, :, :R // 16], 16, axis=3); d["a0"][:, 2:6, :, :R // 2] = d["a"][:, 2:6, :, :R // 2]
    return pack(d)
def setup_inputs_spread(rng):
    d = parts(rng)
    for k in ("s", "m", "a", "a0"):
        n = d[k].shape[3]; d[k] = np.floor(np.exp2(8 * rng.random((N, 8, 1, n))) * rng.random((N, 8, 16, n))).astype(np.int64)
    return pack(d)
def check_inputs(d):
    bad = []
    for k in ("s", "m", "a", "a0"):
        x = np.asarray(d[k]).astype(np.float32)
        if not np.all((x >= 0) & (x <= 255) & (x == np.floor(x))): bad.append("numbers of " + k)
    if np.min(d["lk"]) < 0 or np.max(d["lk"]) > R - 1: bad.append("range of lk")
    if np.min(d["cut0"]) < 2 or np.max(d["cut0"]) > V - 1: bad.append("range of cut0")
    T = N * 8; kid = np.asarray(d["kid"]).astype(np.int64).reshape(T, V); up = np.asarray(d["up"]).astype(np.int64).reshape(T, V)
    if np.min(kid) < -1 or np.max(kid) > V - 1 or np.min(up) < 0 or np.max(up) > V - 1: return bad + ["range of the trees"]
    ar = np.arange(T)[:, None]; n = np.arange(V)[None, :]
    ok = np.all(up[:, :2] == 0) and np.all(kid[:, 1] == -1) and np.all((kid == -1) | ((kid >= 2) & (kid % 2 == 0)))
    ok = ok and np.all(kid[ar, up][:, 2:] == (n - n % 2)[:, 2:]) and np.all(up[:, 0::2] == up[:, 1::2])
    ok = ok and np.all((kid < 0) | (up[ar, np.maximum(kid, 0)] == n))
    jump = [up]; dep = np.where(n == 0, 0, 1) + np.zeros((T, 1), np.int64); K = V.bit_length()
    for k in range(K):
        dep = dep + dep[ar, jump[-1]]; jump.append(jump[-1][ar, jump[-1]])
    if not ok or np.any(jump[-1]): return bad + ["trees"]
    if "range of cut0" in bad: return bad
    c = np.stack([gentries(np.asarray(x)) for x in d["cut0"]]).astype(np.int64).reshape(T, 4 * R, 4); wrong = False
    for i in range(4):
        for j in range(i):
            x, y = c[:, :, i], c[:, :, j]; dx, dy = dep[ar, x], dep[ar, y]
            low = np.where(dx >= dy, x, y); high = np.where(dx >= dy, y, x); dif = np.abs(dx - dy)
            for k in range(K): low = np.where(((dif >> k) & 1) > 0, jump[k][ar, low], low)
            wrong = wrong or bool(np.any(low == high))
    if wrong: bad.append("quads of cut0")
    return bad
def reference(s, m, kid, up, a, a0, lk, cut0):
    def rows(x, n): return np.ascontiguousarray(x.astype(np.float32).astype(np.int64).reshape(N, 8, 16, n).transpose(0, 1, 3, 2))
    sv, mv, av, ka = rows(s, V), rows(m, V), rows(a, R), rows(a0, R)
    kd, pu = kid.astype(np.int64), up.astype(np.int64)
    lv = np.stack([gentries(x) for x in lk]).astype(np.int64).reshape(N, 8, L, R)
    cut = np.stack([gentries(x) for x in cut0]).astype(np.int64).reshape(N, 8, R, 4, 4)
    G3 = np.arange(8)[:, None, None]; G4 = G3[..., None]; E = np.zeros((N, 8, R, 16), np.int64)
    def at(x, i): return np.take_along_axis(x, i, 3)
    for h in range(N):
        newcut = []; newa = []
        for r in range(N):
            b = (r - h) % N; x = av[b]; w = lv[b]
            dist = np.sum(np.abs(x[:, None] - ka[r][G3, w]).reshape(8, L, R, 4, 4), axis=4)
            best = np.argmin(dist, axis=1)
            own = w[G3, best, np.arange(R)[None, :, None]]
            c = cut[r][G3, own, np.arange(4)[None, None, :]]
            xx = x[:, :, None, None, :]
            for step in range(S):
                k = kd[r][G4, c]; p = pu[r][G4, c]
                err = np.where(k >= 0, np.sum(sv[r][G4, c] * xx, axis=4), -1)
                cost = np.sum(sv[r][G4, p] * xx, axis=4)
                i = np.argmax(err, axis=3)[..., None]; free = np.arange(4) != i
                mate = (c[..., None, :] == (c ^ 1)[..., :, None]) & free[..., None, :] & free[..., :, None]
                pair = np.any(mate, axis=4); j = np.argmax(pair, axis=3)[..., None]
                j2 = np.argmax(np.take_along_axis(mate, j[..., None], 3)[..., 0, :], axis=3)[..., None]
                go = np.any(pair, axis=3)[..., None] & (at(cost, j) < at(err, i)); left = at(k, i)
                new = c.copy()
                np.put_along_axis(new, i, left, 3); np.put_along_axis(new, j, at(p, j), 3); np.put_along_axis(new, j2, left + 1, 3)
                c = np.where(go, new, c)
            E[b] += x * np.sum(mv[r][G4, c], axis=(2, 3))
            newcut.append(c); newa.append(x)
        cut = np.stack(newcut); ka = np.stack(newa)
    return {"ye": np.ascontiguousarray(E.transpose(0, 1, 3, 2)).reshape(N, 128, R).astype(np.float32), "yc": np.stack([gtable(x.reshape(8, -1)) for x in cut]).astype(np.float32)}

import numpy as np
from concourse.mybir import dt, AluOpType, ActivationFunctionType
ADD, SUB, MUL, MAX, MIN = AluOpType.add, AluOpType.subtract, AluOpType.mult, AluOpType.max, AluOpType.min
EQ, GT, LT, GE, AND = AluOpType.is_equal, AluOpType.is_gt, AluOpType.is_lt, AluOpType.is_ge, AluOpType.bitwise_and
SHR = AluOpType.arith_shift_right
ACT = ActivationFunctionType
F32, F16, BF, I32, U16 = "float32", "float16", "bfloat16", "int32", "uint16"
N = 4
D5 = [128, 2, 8, 4, 4]
U4 = [128, 2, 8, 4]
SCRATCH = {}
ALIAS = {}


def _m(buf, names, shape, dtype):
    names = names.split()
    for i, n in enumerate(names):
        ALIAS[n] = (buf, i)
    SCRATCH[buf] = ("sbuf", [128, len(names)] + shape[1:], dtype)


def _b(names, shape, dtype, where="sbuf"):
    for n in names.split():
        SCRATCH[n] = (where, shape, dtype)


_b("A0 B0 K0 A1 B1 K1", [128, 2, 2, 8, 4, 4], F32, "psum")
_b("fb", [128, 512], F32, "psum")
_b("mb", [128, 4, 2, 8, 2, 4], F32, "psum")
_b("av0 av1 av2 av3 ak0", [128, 384], BF)
_b("lku0 lku1 lku2 lku3", [128, 96], U16)
_b("lki", [128, 96], I32)
_b("aexp0 aexp1", [128, 4, 1536], BF)
_b("aexq0 aexq1", [128, 2, 1536], BF)
_b("st mt sm", [128, 2048], BF)
_b("w1 w2 num", [128, 4096], BF)
_m("tmp2", "tmpn tmpm", [128, 2048], BF)
_b("tmpu", [128, 1024], BF)
_b("kidi upi", [128, 128], I32)
_b("khi klo kmk", [128, 128], BF)
_b("uhi ulo usg", [128, 64], BF)
_b("upe ubit", [128, 64], I32)
_b("km8", [128, 2048], BF)
_b("k2i", [128, 8, 16], I32)
_b("u2i", [128, 8, 32], I32)
_b("k2h", [128, 128], F16)
_b("u2h u2b", [128, 8, 16], F16)
_m("lk2", "lkl lkr", [128, 128], U16)
_m("lu2", "lup lup2", [128, 64], U16)
_b("cuti", [128, 384], I32)
_b("fw", [128, 384], F32)
_b("fu", [128, 384], U16)
_b("mg", [128, 6144], BF)
_m("ef", "ef0 ef1 ef2 yes", [128, 384], F32)
_b("el1 el2", [128, 384], F32)
_b("el3a el3b", [128, 192], F32)
_m("eh", "ef3a ef3b", [128, 192], F32)
_m("idt", "i16 n1 n2 n3 n4", [128, 128], F16)
_b("ib nb", [128, 128], BF)
_b("i32", [128, 128], F32)
_b("ones4", [128, 2, 8], F32)
_b("g8", [128, 8], F32)
_b("g8i", [128, 128], BF)
_b("pkk", [128, 8, 2], F32)
_b("pick", [128, 4, 8, 4], F32)
_b("qb", [128, 32], BF)
_b("gx", [128, 32], F32)
_b("r2", [128, 48], F16)
_b("pi", [128, 5], I32)
_b("pc", [128, 5], F32)
_b("io16 clm clx", [128, 16], F32)
_b("koff", [128, 96], F32)
_m("gms", "gl gkl gkr", [128, 8], BF)
_m("pks", "pk1 pk0 pkz", [128, 2, 8, 4], BF)
_b("bias1", [128, 64, 4], BF)
_m("cks", "cb cz ck2", [128, 2, 2, 8, 4, 4], BF)
_b("lkf", [128, 96], F32)
_b("lkx", [128, 4, 24, 16], F32)
_b("absd dif", [128, 1536], BF)
_b("dcp", [128, 256], F32)
_b("dm2", [128, 2, 128], F32)
_b("owi owk", [128, 16, 8], I32)
_b("owp", [128, 16, 2, 8], F16)
_b("owl0 owl1", [128, 96], U16)
for _h in "01":
    _b("G" + _h, [128, 768], F32)
    _m("qd" + _h, " ".join(n + _h for n in "cs h16 e v v1 v2 fm px pa pb pd".split()), D5, F16)
    _b("kf" + _h, D5, F32)
    _b("l1" + _h, [128, 2, 96], U16)
    _b("xl" + _h, [128, 96], U16)
    _b("sq%s pm%s" % (_h, _h), [128, 2, 2, 8, 4, 4], BF)
    _b("ph" + _h, [128, 2, 2, 8, 4, 4], F16)
    _b("prA%s prB%s" % (_h, _h), [128, 1536], F32)
    _b("kc%s m2%s" % (_h, _h), [128, 2, 8, 4, 2], F32)
    _b("mx" + _h, U4, F32)
    _b("pr" + _h, [128, 8, 2, 2, 4, 4], F16)
    _b("ng" + _h, [128, 1536], BF)
    _b("uw" + _h, [128, 24, 2, 8, 4], F16)
    _b("uf" + _h, [128, 4, 2, 8, 4], F32)
SEMAPHORES = ["cV", "cS", "cP", "cG", "lsem"] + ["ar%d" % h for h in (1, 2, 3)] + ["er%d" % h for h in (1, 2, 3, 4)] + ["d%d" % i for i in range(60)]
WHOLE = np.s_[:]


def rank_program(g, core, T, topo):
    rank = T.rank_of(core)
    if rank is None:
        return
    ENG = {"V": g.vector, "S": g.scalar, "P": g.tensor, "G": g, "Y": g.sync}
    cnt = {"cV": 0, "cS": 0, "cP": 0, "cG": 0}
    total = {}
    known = {e: {} for e in ENG}
    ops = []
    wr, rd, cache, bank = {}, {}, {}, {}
    ndma = [0]
    prog = []

    def R(name, idx=WHOLE):
        if name in ALIAS:
            ix = idx if isinstance(idx, tuple) else (idx,)
            return (ALIAS[name][0], (ix[0], ALIAS[name][1]) + ix[1:])
        return (name, idx)

    def IND(win, off):
        return ("@", win, off)

    def ap(r):
        if r[0] == "@":
            return ap(r[1]).indirect(ap(r[2]))
        return T[r[0]][r[1]]

    def psum(r):
        return SCRATCH[r[0]][0] == "psum"

    def size(n):
        return 16 * 4096 if n == "num" else int(np.prod(SCRATCH[n][1][1:]))

    def cols(r):
        key = (r[0], repr(r[1]))
        if key not in cache:
            ix = r[1] if isinstance(r[1], tuple) else (r[1],)
            if r[0] == "num":
                rows = np.unique(np.arange(128)[ix[0]] % 16)
                c = np.arange(16 * 4096).reshape(16, 4096)[rows][:, ix[1] if len(ix) > 1 else WHOLE]
            else:
                c = np.arange(size(r[0])).reshape(SCRATCH[r[0]][1][1:])[ix[1:]]
            cache[key] = np.unique(c.reshape(-1))
        return cache[key]

    def parts(rs):
        out = []
        for r in rs:
            if r[0] == "@":
                out += [r[1], r[2]]
            elif r[0] in SCRATCH:
                out.append(r)
        return out

    def hazards(W, L, outs, ins, skip):
        need = set()
        for r in list(ins) + list(outs):
            if not psum(r) and r[0] in W:
                need.update(np.unique(W[r[0]][cols(r)]).tolist())
        for r in outs:
            if psum(r):
                continue
            c, keep = cols(r), []
            for (o, m) in L.get(r[0], []):
                if m[c].any():
                    if not skip(o):
                        need.add(o)
                    m[c] = False
                    if not m.any():
                        continue
                keep.append((o, m))
            L[r[0]] = keep
        need.discard(-1)
        return need

    def note(W, L, o, outs, ins):
        for r in outs:
            if not psum(r):
                if r[0] not in W:
                    W[r[0]] = np.full(size(r[0]), -1)
                W[r[0]][cols(r)] = o
        for r in ins:
            if not psum(r):
                m = np.zeros(size(r[0]), bool)
                m[cols(r)] = True
                L.setdefault(r[0], []).append((o, m))

    def waits(e, outs, ins, queued):
        need = hazards(wr, rd, outs, ins, lambda o: queued and ops[o][0] == e)
        for r in outs + ins:
            if psum(r):
                need.update(o for e2, o in bank.get(r[0], {}).items() if e2 != e)
        k, want = known[e], {}
        for o in need:
            _, s, c, snap = ops[o]
            if k.get(s, 0) < c and (s not in want or want[s][0] < c):
                want[s] = (c, snap)
        for s in list(want):
            if any(s2 != s and want[s2][1].get(s, 0) >= want[s][0] for s2 in want):
                del want[s]
        for s, (c, snap) in want.items():
            if k.get(s, 0) >= c:
                continue
            ENG[e].wait_ge(T.sem[s], c)
            for s2, c2 in snap.items():
                k[s2] = max(k.get(s2, 0), c2)
            k[s] = max(k.get(s, 0), c)

    def issued(e, s, c, snap, outs, ins):
        total[s] = c
        ops.append((e, s, c, snap))
        note(wr, rd, len(ops) - 1, outs, ins)
        for r in outs + ins:
            if psum(r):
                bank.setdefault(r[0], {})[e] = len(ops) - 1

    def issue(o):
        e, outs, ins, a = o["e"], o["o"], o["i"], o["a"]
        if o["k"] == "arr":
            issued(None, a[0], a[1], {}, outs, [])
            return
        if o["k"] == "send":
            waits("G", [], ins, False)
            src, dst, dstname, s = a
            rid, pid = topo.addr(dst, core)
            g.remote_dma(T[dstname][:], ap(src), T.sem[s], T.sem.lsem, pid, rid, topo.mask(core, dst))
            total["lsem"] = total.get("lsem", 0) + len(topo.engines(core, dst))
            return
        waits(e, outs, ins, o["k"] == "op")
        if o["k"] == "dma":
            s = "d%d" % ndma[0]
            ndma[0] += 1
            ENG[e].dma_start(ap(a[0]), ap(a[1])).then_inc(T.sem[s], 16)
            issued(None, s, 16, dict(known[e]), outs, ins)
        else:
            s = "c" + e
            cnt[s] += 1
            a().then_inc(T.sem[s], 1)
            issued(e, s, cnt[s], dict(known[e]), outs, ins)

    def op(e, outs, ins, fn):
        o, i = parts(outs), parts(ins)
        ind = any(r[0] == "@" for r in list(outs) + list(ins))
        if ind:
            d = 60 + 1.7 * len(cols(outs[0]))
        elif e == "P":
            d = 0.52 * max(min(64, len(cols(ins[0]))), len(cols(ins[1]))) * (4 if SCRATCH[ins[0][0]][2] == F32 else 1)
        else:
            n = max(len(cols(r)) // (16 if r[0] == "num" else 1) for r in o + i)
            d = 200 + 2 * n if e == "G" else max(64, n * (2 if e == "V" and len(ins) == 2 and not any(psum(r) for r in i) else 1))
        prog.append({"k": "op", "e": e, "o": o, "i": i, "a": fn, "d": d, "lat": 0})

    def dma(e, out, in_):
        prog.append({"k": "dma", "e": e, "o": parts([out]), "i": parts([in_]), "a": (out, in_), "d": 60, "lat": 2200})

    def arrival(names, s, c, lat):
        prog.append({"k": "arr", "e": "X", "o": [R(n) for n in names.split()], "i": [], "a": (s, c), "d": 0, "lat": lat})

    def send(src, dst, dstname, s):
        prog.append({"k": "send", "e": "G", "o": [R(dstname)], "i": [R(src)], "a": (R(src), dst, dstname, s), "d": 1200, "lat": 0})

    def schedule():
        n = len(prog)
        W, L, hist, pre = {}, {}, {}, []
        for i, o in enumerate(prog):
            S = hazards(W, L, o["o"], o["i"], lambda j: False)
            note(W, L, i, o["o"], o["i"])
            for b in set(r[0] for r in o["o"] + o["i"] if psum(r)):
                hb = hist.setdefault(b, {"P": [], "V": [], "S": []})
                if o["e"] == "P":
                    S.update(hb["P"][-1:] + hb["V"] + hb["S"])
                    hb["V"], hb["S"] = [], []
                else:
                    S.update(hb["P"][-1:] + hb["S" if o["e"] == "V" else "V"][-1:])
                hb[o["e"]].append(i)
            S.discard(i)
            pre.append(S)
        suc = [[] for _ in range(n)]
        for i, S in enumerate(pre):
            for j in S:
                suc[j].append(i)
        WAKE, OV = 130, 35
        gap = lambda i, j: 0 if prog[i]["e"] == prog[j]["e"] == "P" else WAKE
        prio = [0.0] * n
        for i in range(n - 1, -1, -1):
            prio[i] = max([prio[j] + gap(i, j) for j in suc[i]] + [0.0]) + prog[i]["d"] + prog[i]["lat"]
        left, ready = [len(S) for S in pre], [0.0] * n
        avail, t = {e: [] for e in "XYGPSV"}, {e: 0.0 for e in "XYGPSV"}
        for i in range(n):
            if not left[i]:
                avail[prog[i]["e"]].append(i)
        order = []
        while len(order) < n:
            pick = None
            for e in "XYGPSV":
                if avail[e]:
                    now = max(t[e], min(ready[i] for i in avail[e]))
                    if pick is None or now < pick[0]:
                        pick = (now, max((i for i in avail[e] if ready[i] <= now), key=lambda i: (prio[i], -i)), e)
            now, c, e = pick
            avail[e].remove(c)
            end = now + prog[c]["d"] + OV
            if e != "X":
                t[e] = end
            order.append(c)
            for j in suc[c]:
                ready[j] = max(ready[j], end + prog[c]["lat"] + gap(c, j))
                left[j] -= 1
                if not left[j]:
                    avail[prog[j]["e"]].append(j)
        return order

    def tt(out, a, b, o):
        op("V", [out], [a, b], lambda: g.vector.tensor_tensor(ap(out), ap(a), ap(b), o))

    def tc(out, a):
        op("V", [out], [a], lambda: g.vector.tensor_copy(ap(out), ap(a)))

    def ts(out, a, s1, o1, s2=None, o2=None):
        v = lambda x: ap(x) if isinstance(x, tuple) else x
        ins = [a] + [x for x in (s1, s2) if isinstance(x, tuple)]
        if o2 is None:
            op("V", [out], ins, lambda: g.vector.tensor_scalar(ap(out), ap(a), v(s1), None, o1))
        else:
            op("V", [out], ins, lambda: g.vector.tensor_scalar(ap(out), ap(a), v(s1), v(s2), o1, o2))

    def ms(out, c):
        op("V", [out], [], lambda: g.vector.memset(ap(out), c))

    def act(out, a, f=ACT.Copy, bias=0.0, scale=1.0):
        col = isinstance(scale, tuple)
        op("S", [out], [a] + ([scale] if col else []), lambda: g.scalar.activation(ap(out), ap(a), f, bias=bias, scale=ap(scale) if col else scale))

    def mm(out, l, r, start, stop):
        op("P", [out], [l, r], lambda: g.tensor.matmul(ap(out), ap(l), ap(r), start, stop))

    def group(lst):
        for i, (o, l, r) in enumerate(lst):
            mm(o, l, r, i == 0, i == len(lst) - 1)

    def sel(out, in_, pattern, cmp, fill, base, cm):
        op("G", [out], [in_], lambda: g.affine_select(ap(out), ap(in_), pattern, cmp, fill, base, cm))

    def iota(out, pattern, base, cm):
        if SCRATCH[out[0]][2] == I32:
            op("G", [out], [], lambda: g.iota(ap(out), pattern, base, cm))
        else:
            op("G", [out], [], lambda: g.iota(ap(out), pattern, base, cm, allow_small_or_imprecise_dtypes=True))

    s_ = np.s_
    P96 = slice(0, 96)
    I96 = lambda n: R(n, s_[0:96, 0:96])
    cores = list(T.cores)
    nxt = lambda h: cores[(rank + h) % N]

    dma("Y", R("av0"), ("a", s_[:, :]))
    dma("S", R("lki"), ("lk", s_[:, :]))
    dma("Y", R("ak0"), ("a0", s_[:, :]))
    dma("S", R("kidi"), ("kid", s_[:, :]))
    dma("Y", R("cuti"), ("cut0", s_[:, :]))
    dma("S", R("upi"), ("up", s_[:, :]))
    dma("Y", R("st"), ("s", s_[:, :]))
    ms(R("i16"), 1.0)
    sel(R("i16"), R("i16"), [[-1, 128]], EQ, 0.0, 0, 1)
    ms(R("qb"), 2048.0)
    ms(R("gx"), 1.0)
    sel(R("qb"), R("qb"), [[-16, 8], [-4, 4]], GE, 0.0, 0, 1)
    sel(R("qb"), R("qb"), [[16, 8], [4, 4]], GE, 0.0, 3, -1)
    iota(R("pi", s_[:, 0:1]), [[0, 1]], 0, 1)
    sel(R("gx"), R("gx"), [[-16, 8], [0, 4]], GE, 0.0, 0, 1)
    sel(R("gx"), R("gx"), [[16, 8], [0, 4]], GE, 0.0, 15, -1)
    iota(R("koff"), [[512, 4], [0, 24]], 0, 0)
    iota(R("io16"), [[1, 16]], 0, 0)
    ms(R("r2"), 1.0)
    sel(R("r2"), R("r2"), [[-2, 48]], GE, 0.0, 0, 1)
    sel(R("r2"), R("r2"), [[2, 48]], GE, 0.0, 1, -1)
    ms(R("pick"), 1.0)
    sel(R("pick"), R("pick"), [[-4, 4], [-16, 8], [-1, 4]], EQ, 0.0, 0, 1)
    ms(R("ones4"), 4.0)
    sel(R("ones4"), R("ones4"), [[0, 2], [-16, 8]], GE, 0.0, 0, 1)
    sel(R("ones4"), R("ones4"), [[0, 2], [16, 8]], GE, 0.0, 15, -1)
    iota(R("bias1"), [[0, 64], [-1, 4]], 3, 0)
    tc(R("lku0"), R("lki"))
    for h in (1, 2, 3):
        send("av0", nxt(h), "av%d" % h, "ar%d" % h)
        send("lku0", nxt(h), "lku%d" % h, "ar%d" % h)
        arrival("av%d lku%d" % (h, h), "ar%d" % h, 2 * len(topo.engines(nxt(-h), core)), 8000)
    ts(R("pi", s_[:, 1:2]), R("pi", s_[:, 0:1]), 1, AND)
    ts(R("pi", s_[:, 2:3]), R("pi", s_[:, 0:1]), 1, SHR, 7, AND)
    ts(R("pi", s_[:, 3:4]), R("pi", s_[:, 0:1]), 2, SHR, 1, AND)
    ts(R("pi", s_[:, 4:5]), R("pi", s_[:, 0:1]), 15, AND)
    tc(R("pc", s_[:, 0:1]), R("pi", s_[:, 1:2]))
    ts(R("pc", s_[:, 1:2]), R("pi", s_[:, 1:2]), -1.0, MUL, 1.0, ADD)
    tc(R("pc", s_[:, 2:3]), R("pi", s_[:, 2:3]))
    ts(R("pc", s_[:, 3:4]), R("pi", s_[:, 3:4]), 2048.0, MUL)
    tc(R("pc", s_[:, 4:5]), R("pi", s_[:, 4:5]))
    ts(R("clm"), R("io16"), R("pc", s_[:, 2:3]), EQ)
    ts(R("clx"), R("io16"), R("pc", s_[:, 4:5]), EQ)

    def dist(h):
        av, lku, ow = "av%d" % h, "lku%d" % h, "owl%d" % (h % 2)
        ak = "ak0" if h == 0 else "av%d" % (h - 1)
        for k in range(4):
            c = s_[:, 384 * k:384 * k + 384]
            i = IND(R(ak, s_[:, 0:384]), R(lku, s_[:, 24 * k:24 * k + 24]))
            if h == 0:
                tt(R("dif", c), i, R(av), SUB)
                act(R("absd", c), R("dif", c), ACT.Abs)
            else:
                act(R("dif", c), i)
        for k in range(4 if h else 0):
            c = s_[:, 384 * k:384 * k + 384]
            group([(R("fb", s_[:, 0:384]), R("ib"), R("dif", c)), (R("fb", s_[:, 0:384]), R("nb"), R(av))])
            act(R("absd", c), R("fb", s_[:, 0:384]), ACT.Abs)
        ts(R("lkf"), R(lku), 1.0, MUL)
        tt(R("lkf"), R("lkf"), R("koff"), ADD)
        for cl in range(16):
            act(R("lkx", s_[:, :, :, cl]), R("lkf"), ACT.Copy, 0.0, R("clx", s_[:, cl:cl + 1]))
        for k in range(4):
            for H in (0, 1):
                for bl in (0, 1):
                    o = R("mb", s_[0:96, k, H, :, bl, :])
                    j = 2 * H + bl
                    group([(o, R("absd", s_[:, 384 * k + 96 * j:384 * k + 96 * j + 96]), R("qb")),
                           (o, R("lkx", s_[:, k, 6 * j:6 * j + 6, :]), R("gx"))])
        act(R("dcp", s_[P96, :]), R("mb", s_[P96, 2:4, :, :, :, :]))
        tt(R("dm2", s_[P96, :, :]), R("mb", s_[P96, 0:2, :, :, :, :]), R("dcp", s_[P96, :]), MIN)
        tt(R("owi", s_[P96]), R("dm2", s_[P96, 0, :]), R("dm2", s_[P96, 1, :]), MIN)
        ts(R("owk", s_[P96]), R("owi", s_[P96]), 511, AND)
        for b in (0, 1):
            ts(R("owp", s_[P96, :, b, :]), R("owk", s_[P96]), R("pc", s_[P96, 1 - b:2 - b]), MUL)
        for H in (0, 1):
            mm(R("mb", s_[:, 0, H, 0:6, :, :]), R("owp", s_[P96, 8 * H:8 * H + 8, :, :]), R("r2", s_[P96, :]), True, True)
        tc(R(ow), R("mb", s_[:, 0, :, 0:6, :, :]))

    def inherit(h, H):
        x = str(H)
        A, G = "A" + x, "G" + x
        act(R(G), IND(R("fw", s_[:, 0:384]), R("owl%d" % (h % 2), s_[:, 48 * H:48 * H + 48])))
        for bl in (0, 1):
            for q in range(4):
                mm(R(A, s_[P96, 0, bl, :, q, :]), R(G, s_[:, 4 * bl + q::8]), R("pick", s_[:, q, :, :]), True, True)
        tc(R("cs" + x, s_[P96]), R(A, s_[P96, 0]))
        for bl in (0, 1):
            mm(R(A, s_[:, 1, bl, 0:6, :, :]), R("cs" + x, s_[P96, bl]), I96("i16"), True, True)
        tc(R("l1" + x), R(A, s_[:, 1, :, 0:6, :, :]))

    def gather1(h, H):
        x = str(H)
        A, B, K = "A" + x, "B" + x, "K" + x
        ax, h16 = "aexp%d" % (h % 2), "h16" + x
        for bl, pr in ((0, "prA" + x), (1, "prB" + x)):
            tt(R(pr), IND(R("sm", s_[:, 0:2048]), R("l1" + x, s_[:, bl, :])), R(ax, s_[:, 2 * H + bl, :]), MUL)
        ts(R(h16, s_[P96]), R("cs" + x, s_[P96]), 0.5, MUL, 1023.75, ADD)
        ends = ((R(B, s_[P96, 0, :, :, :, 0:3]), R(A, s_[P96, 1, :, :, :, 0:3]), 3, 1), (R(B, s_[P96, 0, :, :, :, 3:4]), R(A, s_[P96, 1, :, :, :, 3:4]), 1, 3),
                (R(B, s_[P96, 1, :, :, :, 0:2]), R(B, s_[P96, 1, :, :, :, 2:4]), 2, 2))
        for (o, o2, n, dl) in ends:
            group([(o, I96("i16"), R(h16, s_[P96, :, :, :, 0:n])), (o, I96("n1"), R(h16, s_[P96, :, :, :, dl:dl + n]))])
        for (o, o2, n, dl) in ends:
            mm(o2, I96("i16"), R(h16, s_[P96, :, :, :, 0:n]), True, True)
        for i in (s_[P96, 0], s_[P96, 1, :, :, :, 0:2]):
            act(R("sq" + x, i), R(B, i), ACT.Square)
            act(R("pm" + x, i), R("sq" + x, i), ACT.Relu, 1.0, -1.0)
        tt(R("ph" + x, s_[P96, 0]), R(A, s_[P96, 1]), R("pm" + x, s_[P96, 0]), MUL)
        tt(R("ph" + x, s_[P96, 1, :, :, :, 0:2]), R(B, s_[P96, 1, :, :, :, 2:4]), R("pm" + x, s_[P96, 1, :, :, :, 0:2]), MUL)
        lst = [(R(K, s_[P96, 0]), I96("ib"), R("bias1", s_[P96]))]
        for bl, pr in ((0, "prA" + x), (1, "prB" + x)):
            for q in range(4):
                for t in range(4):
                    lst.append((R(K, s_[P96, 0, bl, :, q, t]), R(pr, s_[:, 4 * q + t::16]), R("ones4", s_[:, 0, :])))
        group(lst)
        sl = (((0, 1), 0, 0), ((1, 2), 0, 1), ((2, 3), 0, 2), ((0, 3), 0, 3), ((0, 2), 1, 0), ((1, 3), 1, 1))
        for t in range(4):
            group([(R(B, s_[P96, 0, :, :, :, t]), I96("i16"), R("ph" + x, s_[P96, i, :, :, :, j])) for tu, i, j in sl if t not in tu])

    def logic1a(h, H):
        x = str(H)
        A, B, K = "A" + x, "B" + x, "K" + x
        e, pr = "e" + x, "pr" + x
        tc(R("kc" + x, s_[P96]), R(K, s_[P96, 0, :, :, :, 2:4]))
        tt(R("m2" + x, s_[P96]), R(K, s_[P96, 0, :, :, :, 0:2]), R("kc" + x, s_[P96]), MAX)
        tt(R("mx" + x, s_[P96]), R("m2" + x, s_[P96, :, :, :, 0]), R("m2" + x, s_[P96, :, :, :, 1]), MAX)
        for t in range(4):
            tt(R(e, s_[P96, :, :, :, t]), R(K, s_[P96, 0, :, :, :, t]), R("mx" + x, s_[P96]), EQ)
        for l, src in ((0, B), (1, A)):
            for bl in (0, 1):
                tt(R(pr, s_[P96, :, bl, l, :, :]), R(src, s_[P96, 0, bl]), R(e, s_[P96, bl]), MUL)
        o = R(B, s_[:, 1, 0, 0:6, :, :])
        group([(o, R(pr, s_[P96, :, :, :, :, t]), I96("i16")) for t in range(4)])
        for bl in (0, 1):
            group([(R(A, s_[P96, 1, bl, :, 0:2, :]), I96("i16"), R(pr, s_[P96, :, bl, :, :, t])) for t in range(4)])
        ts(R("xl" + x), o, R("pc", s_[:, 3:4]), ADD)

    def uw(x, i):
        return R("uw" + x, s_[P96, i])

    def logic1b(h, H):
        x = str(H)
        A, K = "A" + x, "K" + x
        U = lambda n, t: R(n + x, s_[P96, :, :, :, t])
        for t in range(4):
            tt(U("v", t), R(A, s_[P96, 1, :, :, 0, :]), U("h16", t), EQ)
        ts(uw(x, 0), R(A, s_[P96, 1, :, :, 0, :]), -1024.0, ADD)
        tc(uw(x, 1), R(A, s_[P96, 1, :, :, 1, :]))
        tt(U("v2", 1), U("v", 1), U("v", 0), MUL)
        tt(U("v2", 2), U("v", 2), U("v", 3), GT)
        tt(U("v1", 1), U("v", 1), U("v", 0), GT)
        tt(U("v1", 2), U("v", 2), U("v", 3), MUL)
        cf = R(K, s_[P96, 1, :, :, 3, :])
        group([(cf, I96("ib"), R("cz", s_[P96, 0, :, :, 0, :]))] + [(cf, I96("i16"), U("cs", t)) for t in range(4)] + [(cf, I96("n1"), uw(x, 1)), (cf, I96("n4"), uw(x, 0))])
        V1 = {0: U("v", 0), 1: U("v1", 1), 2: U("v1", 2)}
        V2 = {1: U("v2", 1), 2: U("v2", 2), 3: U("v", 3)}
        for t in (1, 2, 3):
            tt(uw(x, 2 + t), R(A, s_[P96, 0, :, :, :, t]), V2[t], MUL)
        tc(uw(x, 2), cf)
        for t in range(4):
            tt(U("fm", t), cf, U("cs", t), EQ)
        tt(R("kf" + x, s_[P96]), R(K, s_[P96, 0]), R("fm" + x, s_[P96]), MUL)
        return V1, V2

    def gather2(h, H, V1, V2):
        x = str(H)
        A, B, K = "A" + x, "B" + x, "K" + x
        ax, ng = "aexq%d" % (h % 2), "ng" + x
        U = lambda n, t: R(n + x, s_[P96, :, :, :, t])
        for w, pr in (("w1", "prA" + x), ("w2", "prB" + x)):
            tt(R(pr), IND(R(w, s_[:, 0:4096]), R("xl" + x)), R(ax, s_[:, H, :]), MUL)
        act(R(ng), IND(R("num", s_[:, 0:4096]), R("xl" + x)))
        reg = lambda hf, r: R(K, s_[P96, hf, :, :, r, :])
        sc = ["i16", "n1", "n2", "n3"]
        lst = [(R(K, s_[P96]), I96("ib"), R("ck2", s_[P96]))]
        for t in (1, 2, 3):
            lst += [(reg(0, 2), I96(sc[t]), U("e", t)), (reg(0, 3), I96(sc[t]), V2[t]), (reg(1, 2), I96(sc[t]), U("e", t)), (reg(1, 2), I96(sc[t]), V2[t])]
        for t in (1, 2):
            lst += [(reg(0, 1), I96(sc[t]), V1[t]), (reg(1, 2), I96(["", "n2", "n4"][t]), V1[t])]
        for t in range(4):
            lst.append((reg(1, 1), I96("i32"), R("kf" + x, s_[P96, :, :, :, t])))
        for w, pr in ((0, "prA" + x), (1, "prB" + x)):
            for bl in (0, 1):
                for q in range(4):
                    if w == 0:
                        lst.append((R(K, s_[P96, 0, bl, :, 0:2, q]), R(pr, s_[:, 8 * bl + q::16]), R("pkk")))
                    else:
                        lst.append((R(K, s_[P96, 1, bl, :, 0, q]), R(pr, s_[:, 8 * bl + q::16]), R("ones4", s_[:, 0, :])))
                    lst.append((R(K, s_[P96, 0, bl, :, 2 + w, q]), R(pr, s_[:, 8 * bl + 4 + q::16]), R("ones4", s_[:, 0, :])))
        lb = [(R(B, s_[P96]), I96("ib"), R("cb", s_[P96]))]
        for bl in (0, 1):
            for q in range(4):
                o = R(B, s_[P96, :, bl, :, :, q])
                lb += [(o, R(ng, s_[:, 8 * bl + 4 + q::16]), R("pk1")), (o, R(ng, s_[:, 8 * bl + q::16]), R("pk0"))]
        rb = lambda hf, r: R(B, s_[P96, hf, :, :, r, :])
        lb += [(rb(0, 0), I96("n1"), uw(x, 1)), (rb(1, 3), I96("n4"), uw(x, 0))]
        for i in (3, 4, 5):
            lb += [(rb(1, 3), I96("i16"), uw(x, i)), (rb(0, 2), I96("n1"), uw(x, i))]
        group(lb)
        la = [(R(A, s_[P96, 1, :, :, 2:4, :]), I96("ib"), R("cz", s_[P96, 1, :, :, 2:4, :]))]
        for bl in (0, 1):
            for q in range(4):
                la.append((R(A, s_[P96, 1, bl, :, 2:4, q]), R(ng, s_[:, 8 * bl + q::16]), R("pkz", s_[:, 0, :, 0:2])))
        for r in (2, 3):
            la.append((R(A, s_[P96, 1, :, :, r, :]), I96("n1"), uw(x, 2)))
        group(la)
        group(lst)

    def logic2(h, H, V1, V2):
        x = str(H)
        A, B, K = "A" + x, "B" + x, "K" + x
        U = lambda n, t: R(n + x, s_[P96, :, :, :, t])
        kr = lambda hf, r: R(K, s_[P96, hf, :, :, r, :])
        rb = lambda hf, r: R(B, s_[P96, hf, :, :, r, :])
        ra = lambda r: R(A, s_[P96, 1, :, :, r, :])
        uf = lambda i: R("uf" + x, s_[P96, i])
        G1, G2, W, O, P2, GW, GN, WKD, Q, OQ = 6, 7, 8, 9, 10, 11, 12, 13, 14, 15
        ts(uw(x, P2), ra(3), 0.0, EQ)
        ts(uw(x, O), kr(1, 2), 0.0, GT)
        tc(uf(0), kr(0, 1))
        tc(uf(1), kr(0, 2))
        tt(uw(x, G1), kr(0, 0), R("mx" + x, s_[P96]), LT)
        tt(uf(2), kr(1, 1), uf(0), MAX)
        tt(uf(3), kr(0, 3), uf(1), MAX)
        tt(uw(x, W), kr(0, 3), uf(1), GT)
        tt(uf(0), kr(1, 0), uf(2), MAX)
        tt(uw(x, P2), uw(x, P2), uw(x, G1), MUL)
        tt(uw(x, WKD), rb(1, 0), uw(x, W), MUL)
        tt(uw(x, G2), uf(3), uf(0), GT)
        tt(uw(x, Q), rb(1, 2), uw(x, WKD), SUB)
        tt(uw(x, G2), uw(x, G2), uw(x, P2), MUL)
        tt(uw(x, OQ), uw(x, O), uw(x, Q), MUL)
        tt(uw(x, GW), uw(x, G2), uw(x, W), MUL)
        tt(uf(1), uw(x, WKD), uw(x, OQ), ADD)
        tt(uw(x, GN), uw(x, G2), uw(x, GW), SUB)
        tt(uw(x, 16), ra(2), uw(x, OQ), SUB)
        tt(uw(x, 17), rb(1, 1), uf(1), ADD)
        tt(uw(x, 18), rb(0, 0), uw(x, G1), MUL)
        tt(uw(x, 19), rb(0, 2), uw(x, G1), MUL)
        tt(uw(x, 20), rb(1, 3), uw(x, G1), MUL)
        tt(uw(x, 21), rb(0, 1), uw(x, GN), MUL)
        tt(uw(x, 22), rb(0, 3), uw(x, GW), MUL)
        tt(uw(x, 16), uw(x, 16), uw(x, G2), MUL)
        tt(uw(x, 17), uw(x, 17), uw(x, G2), MUL)
        go = lambda r: R(A, s_[P96, 0, :, :, r, :])
        group([(go(0), I96("i16"), uw(x, 18)), (go(0), I96("i16"), uw(x, 21))])
        group([(go(2), I96("i16"), uw(x, 19)), (go(2), I96("i16"), uw(x, 22))])
        mm(go(3), I96("i16"), uw(x, 16), True, True)
        group([(go(1), I96("i16"), uw(x, 20)), (go(1), I96("i16"), uw(x, 17))])
        for t in range(4):
            tt(U("px", t), go(0), U("e", t), MUL)
        for t in (1, 2, 3):
            tt(U("pb", t), go(2), V2[t], MUL)
        for t in range(4):
            tt(U("pd", t), go(3), U("fm", t), MUL)
        for t in (0, 1, 2):
            tt(U("pa", t), go(1), V1[t], MUL)
        for bl in (0, 1):
            o = R("fb", s_[:, 192 * H + 96 * bl:192 * H + 96 * bl + 96])
            group([(o, R(n + x, s_[P96, bl]), I96("i16")) for n in ("cs", "px", "pb", "pd", "pa")])
        c = s_[:, 192 * H:192 * H + 192]
        act(R("fw", c), R("fb", c))
        tc(R("fu", c), R("fb", c))

    def out_half(h, H):
        n = "3" + "ab"[H]
        act(R("ef" + n), R("mb", s_[:, 2 * H:2 * H + 2, :, 0:6, :, :]))
        send("ef" + n, nxt(-h), "el" + n, "er%d" % (3 + H))
        arrival("el" + n, "er%d" % (3 + H), len(topo.engines(nxt(h), core)), 4000)

    def msum(h, last=False):
        for b in range(4):
            o = R("mg", s_[:, 1536 * b:1536 * b + 1536])
            i = IND(R("mt", s_[:, 0:2048]), R("fu", s_[:, 96 * b:96 * b + 96]))
            if last and b % 2 == 0:
                tc(o, i)
            else:
                act(o, i)
        for b in range(4):
            if last and b == 2:
                out_half(h, 0)
            group([(R("mb", s_[:, b, :, 0:6, :, :]), R("ib"), R("mg", s_[:, 1536 * b + t:1536 * b + 1536:16])) for t in range(16)])
        if last:
            out_half(h, 1)
            return
        act(R("ef%d" % h), R("mb", s_[:, :, :, 0:6, :, :]))
        if h:
            send("ef%d" % h, nxt(-h), "el%d" % h, "er%d" % h)
            arrival("el%d" % h, "er%d" % h, len(topo.engines(nxt(h), core)), 4000)

    def expand(h):
        for t in range(16):
            if h == 0:
                tc(R("aexp0", s_[:, :, t::16]), R("av0"))
            else:
                sel(R("aexp%d" % (h % 2), s_[:, :, t::16]), R("av%d" % h), [[0, 384]], EQ, 0.0, 0, 0)
        for H in (0, 1):
            for t in range(16):
                j = 192 * H + 96 * (t // 8)
                sel(R("aexq%d" % (h % 2), s_[:, H, t::16]), R("av%d" % h, s_[:, j:j + 96]), [[0, 96]], EQ, 0.0, 0, 0)

    ts(R("fw"), R("cuti"), 1.0, MUL)
    dist(0)
    ts(R("kmk"), R("kidi"), 0.0, GE)
    dma("Y", R("km8", s_[0:8, :]), R("kmk"))
    for gg in range(8):
        dma("Y", R("k2i", s_[:, gg, :]), ("kid", s_[gg, :]))
        dma("S", R("u2i", s_[0:64, gg, :]), ("up", s_[gg, :]))
    dma("Y", R("mt"), ("m", s_[:, :]))
    tc(R("khi"), R("kidi"))
    ms(R("num"), 0.0)
    ms(R("w1", s_[:, 0:1024]), 255.0)
    ms(R("w2", s_[:, 0:1024]), 255.0)
    tt(R("klo"), R("kidi"), R("khi"), SUB)
    tc(R("uhi"), R("upi", s_[:, 0:128:2]))
    tc(R("upe"), R("upi", s_[:, 0:128:2]))
    tt(R("ulo"), R("upi", s_[:, 0:128:2]), R("uhi"), SUB)
    ts(R("ubit"), R("upe"), 1, AND)
    ts(R("usg"), R("ubit"), -2.0, MUL, 1.0, ADD)
    dma("Y", R("num", s_[0::16, 2048:4096]), R("khi"))
    dma("S", R("num", s_[1::16, 2048:4096]), R("klo"))
    dma("Y", R("num", s_[0::16, 1024:2048]), R("uhi"))
    dma("S", R("num", s_[1::16, 1024:2048]), R("ulo"))
    dma("Y", R("num", s_[4::16, 1024:2048]), R("usg"))
    for k, n in enumerate(("n1", "n2", "n3", "n4")):
        ts(R(n, s_[P96, :]), R("i16", s_[P96, :]), -1.0 - k, MUL)
    tc(R("ib"), R("i16"))
    tc(R("i32"), R("i16"))
    ts(R("nb"), R("i16"), -1.0, MUL)
    ms(R("g8i"), 1.0)
    sel(R("g8i"), R("g8i"), [[1, 128]], GE, 0.0, 0, -16)
    sel(R("g8i"), R("g8i"), [[-1, 128]], GE, 0.0, 15, 16)
    for i, bk in enumerate(("A1", "B1", "K1", "K0")):
        mm(R(bk), R("g8i", s_[0:8, :]), R("km8", s_[0:8, 512 * i:512 * i + 512]), True, True)
        tt(R("sm", s_[:, 512 * i:512 * i + 512]), R(bk), R("st", s_[:, 512 * i:512 * i + 512]), MUL)
    tc(R("k2h"), R("k2i"))
    tc(R("u2h", s_[0:64]), R("u2i", s_[0:64, :, 0:32:2]))
    ts(R("u2b", s_[0:64]), R("u2h", s_[0:64]), 0.5, MUL, 1023.75, ADD)
    mm(R("B0", s_[:, 0, 0]), R("k2h"), R("i16"), True, True)
    mm(R("B0", s_[:, 0, 1, 0:4]), R("u2h", s_[0:64]), R("i16", s_[0:64, 0:64]), True, True)
    mm(R("B0", s_[:, 0, 1, 4:8]), R("u2b", s_[0:64]), R("i16", s_[0:64, 0:64]), True, True)
    tc(R("lkl"), R("B0", s_[:, 0, 0]))
    ts(R("lkr"), R("B0", s_[:, 0, 0]), 1.0, ADD)
    tc(R("lup"), R("B0", s_[:, 0, 1, 0:4]))
    tc(R("lup2"), R("B0", s_[:, 0, 1, 4:8]))
    inherit(0, 0)
    expand(0)
    inherit(0, 1)
    act(R("tmpn"), IND(R("num", s_[:, 2048:4096]), R("lkl")))
    act(R("tmpm"), IND(R("num", s_[:, 2048:4096]), R("lkr")))
    act(R("tmpu"), IND(R("num", s_[:, 0:2048]), R("lup2")))
    for i in (0, 1):
        dma("Y", R("num", s_[2 + i::16, 2048:4096]), R("tmpn", s_[i::16, :]))
        dma("Y", R("num", s_[4 + i::16, 2048:4096]), R("tmpm", s_[i::16, :]))
        dma("Y", R("num", s_[2 + i::16, 1024:2048]), R("tmpu", s_[i::16, :]))
    tc(R("g8"), R("ones4", s_[:, 0, :]))
    for k, n in enumerate(("gl", "gkl", "gkr")):
        ts(R(n), R("g8"), 0.25, MUL, R("clm", s_[:, k:k + 1]), MUL)
    for n in ("pk1", "pk0", "pkz", "cb", "cz", "ck2"):
        ms(R(n), 0.0)
    for t in (0, 1):
        tc(R("pkk", s_[:, :, t]), R("g8"))
    for (n, hf, r, pos, neg) in (("pk1", 0, 0, "gl", None), ("pk1", 0, 1, "gkl", "gl"), ("pk1", 0, 2, "gl", None), ("pk1", 0, 3, "gkr", "gl"),
                                 ("pk1", 1, 0, "gkr", "gkl"), ("pk1", 1, 1, "gkl", None), ("pk1", 1, 2, None, "gkl"),
                                 ("pk0", 1, 1, None, "gl"), ("pk0", 1, 2, "gkl", None), ("pk0", 1, 3, "gl", None), ("pkz", 0, 0, "gkl", None)):
        o = R(n, s_[:, hf, :, r])
        if neg is None:
            tc(o, R(pos))
        elif pos is None:
            ts(o, R(neg), -1.0, MUL)
        else:
            tt(o, R(pos), R(neg), SUB)
    tt(R("pkz", s_[:, 0, :, 1]), R("gl"), R("gkr"), ADD)
    for (hf, r, c) in ((0, 2, 1.0), (0, 3, -1.0), (1, 1, 1.0), (1, 2, -1.0), (1, 3, -1.0)):
        ms(R("cb", s_[:, hf, :, :, r, :]), c)
    ms(R("cz", s_[:, 0, :, :, 0, :]), -1.0)
    ms(R("ck2", s_[:, 0]), 3.0)
    ms(R("ck2", s_[:, 1, :, :, 0, :]), 3.0)
    ms(R("ck2", s_[:, 1, :, :, 2, :]), 6.0)
    for x in "01":
        ms(R("pa" + x, s_[:, :, :, :, 3]), 0.0)
        ms(R("pb" + x, s_[:, :, :, :, 0]), 0.0)
    for h in range(N):
        if h:
            inherit(h, 0)
            inherit(h, 1)
        gather1(h, 0)
        gather1(h, 1)
        if h:
            msum(h - 1)
        else:
            act(R("w1", s_[:, 2048:4096]), IND(R("sm", s_[:, 0:2048]), R("lkl")))
            act(R("w1", s_[:, 1024:2048]), IND(R("sm", s_[:, 0:2048]), R("lup")))
            act(R("w2", s_[:, 2048:4096]), IND(R("sm", s_[:, 0:2048]), R("lkr")))
            act(R("w2", s_[:, 1024:2048]), IND(R("w1", s_[:, 0:2048]), R("lup2")))
        logic1a(h, 0)
        logic1a(h, 1)
        V = {}
        for H in (0, 1):
            V[H] = logic1b(h, H)
            gather2(h, H, *V[H])
        if h == 0:
            dist(1)
        if h + 1 < N:
            expand(h + 1)
        logic2(h, 0, *V[0])
        logic2(h, 1, *V[1])
        if h + 2 < N:
            dist(h + 2)
    dma("Y", ("yc", s_[:, :]), R("fw"))
    tt(R("ef0"), R("ef0"), R("el1"), ADD)
    tt(R("ef0"), R("ef0"), R("el2"), ADD)
    msum(3, True)
    for H in (0, 1):
        c = s_[:, 192 * H:192 * H + 192]
        tt(R("yes", c), R("ef0", c), R("el3" + "ab"[H]), ADD)
        tt(R("yes", c), R("yes", c), R("av0", c), MUL)
        dma("Y", ("ye", c), R("yes", c))
    for i in schedule():
        issue(prog[i])
    for s, c in sorted(total.items()):
        if known["G"].get(s, 0) < c:
            g.wait_ge(T.sem[s], c)
